import numpy as np
import ml_dtypes


def mxq(x, axis, fmt="e4m3"):
    dtype, down = {"e4m3": (ml_dtypes.float8_e4m3fn, 7), "e5m2": (ml_dtypes.float8_e5m2, 14)}[fmt]
    v = np.moveaxis(np.asarray(x, np.float32).astype(ml_dtypes.bfloat16).astype(np.float64), axis, -1)
    blocks = v.reshape(v.shape[:-1] + (-1, 32))
    amax = np.abs(blocks).max(-1, keepdims=True)
    byte = np.maximum(np.where(amax > 0, np.frexp(amax)[1] - 1 + 127, 0) - down, 1)
    scale = np.exp2(byte - 127.0)
    codes = (blocks / scale).astype(np.float32).astype(dtype).astype(np.float64)
    return np.moveaxis((codes * scale).reshape(v.shape), -1, axis)


WIDE = False


def mx_kscale(k):
    if not WIDE:
        return np.ones(k)
    levels = np.array([10, -10, 5, -5, 0])
    if k % 512:
        return np.exp2(np.random.permutation(np.resize(levels, k // 32))).repeat(32)
    a = np.empty((k // 512, 16))
    for p in range(k // 512):
        a[p, :8] = np.random.permutation(np.resize(levels, 8))
        for g in range(8):
            far = levels[np.abs(levels - a[p, g]) >= 10]
            a[p, g + 8] = far[np.random.randint(len(far))]
    return np.exp2(a.ravel()).repeat(32)


def f64(x):
    return np.asarray(x).astype(np.float64)


def striped(idx):
    return np.tile(idx.reshape(-1, 16).T, (8, 1)).astype(np.uint16)


def unstriped(offs):
    return offs[:16].T.reshape(-1).astype(np.int64)


K, T, E, C, N = 2048, 768, 4, 128, 384


def by_expert(wq, xq):
    return np.concatenate([wq[e].T @ xq[:, e * C:(e + 1) * C] for e in range(E)], axis=1)


def setup_inputs():
    n = np.random.standard_normal
    s = mx_kscale(K)[:, None]
    return {
        "xT": (n((K, T)) * s).astype(np.float32),
        "xr": n((N, T)).astype(np.float32),
        "w": (n((E, K, N)) / np.sqrt(K) / s[None]).astype(np.float32),
        "b": (0.3 * n((N, E))).astype(np.float32),
        "gate": np.tile(np.random.uniform(0.2, 1.0, E * C), (N, 1)).astype(np.float32),
        "offs": striped(np.random.permutation(T)[:E * C]),
    }


def reference(xT, xr, w, b, gate, offs):
    idx = unstriped(offs)
    xq = mxq(f64(xT)[:, idx], 0, "e4m3")
    y = by_expert(mxq(f64(w), 1, "e4m3"), xq)
    y = y + np.repeat(f64(b), C, axis=1)
    out = f64(xr).copy()
    out[:, idx] += f64(gate) * y
    return out

@@ -1,0 +1,175 @@
+import concourse.mybir as mybir
+
+K, T, E, C, N = 2048, 768, 4, 128, 384
+S = E * C
+
+F32 = mybir.dt.float32
+BF16 = mybir.dt.bfloat16
+U32 = mybir.dt.uint32
+U16 = mybir.dt.uint16
+U8 = mybir.dt.uint8
+FP8X4 = mybir.dt.float8_e4m3fn_x4
+COPY = mybir.ActivationFunctionType.Copy
+IDENTITY = mybir.ActivationFunctionType.Identity
+MULT = mybir.AluOpType.mult
+
+P = 128
+PACK = 4
+K_PASS = P * PACK
+PASSES = K // K_PASS
+BLOCKS = N // P
+
+FLOPS = 2 * S * K * N
+BYTES = 4 * (K * T + 2 * N * T + E * K * N + N * E + S) + 2 * S
+
+
+def interleave(copy, grouped, raw, lo, hi):
+    copy(
+        grouped[:, PACK * lo : PACK * hi].rearrange("p (c i t) -> p c t i", i=4, t=PACK),
+        raw[:, :, lo:hi].rearrange("p t (c i) -> p c t i", i=4),
+    )
+
+
+def tile_moe_res_lin_bias_kernel(tc, xT, xr, w, b, gate, offs, out):
+    nc = tc.nc
+    with (
+        tc.tile_pool(name="held", bufs=1) as held,
+        tc.tile_pool(name="xin", bufs=4) as xin,
+        tc.tile_pool(name="win", bufs=12) as w_in,
+        tc.tile_pool(name="xgrp", bufs=2) as xgrp,
+        tc.tile_pool(name="wgrp", bufs=4) as wgrp,
+        tc.tile_pool(name="wq", bufs=8) as wq,
+        tc.tile_pool(name="ypool", bufs=4) as ypool,
+        tc.psum_pool(name="acc", bufs=2) as psum,
+    ):
+        offsets = held.tile([P, S // 16], U16, name="offsets")
+        bias = held.tile([P, BLOCKS, E], F32, name="bias")
+        gates = held.tile([P, S], F32, name="gates")
+        residual = [held.tile([P, T], F32, name=f"residual{c}") for c in range(BLOCKS)]
+        window = [held.tile([P, T], F32, name=f"window{c}") for c in range(BLOCKS)]
+        result = [held.tile([P, T], F32, name=f"result{c}") for c in range(BLOCKS)]
+        x_codes = [held.tile([P, T], U32, name=f"x_codes{a}", align_bytes=64) for a in range(PASSES)]
+        x_scales = held.tile([P, T], U8, name="x_scales", align_bytes=64)
+        slot_codes = [held.tile([P, S], U32, name=f"slot_codes{a}", align_bytes=64) for a in range(PASSES)]
+        slot_scales = held.tile([P, S], U8, name="slot_scales", align_bytes=64)
+
+        nc.gpsimd.memset(x_scales[:], 0)
+        for c in range(BLOCKS):
+            nc.gpsimd.memset(window[c][:], 0.0)
+
+        vcopy = lambda o, i: nc.vector.tensor_copy(o, i)
+        scopy = lambda o, i: nc.scalar.activation(o, i, COPY)
+
+        raws, grps = {}, {}
+        w_codes, w_scales, acc = {}, {}, {}
+
+        def load(ch):
+            if ch[0] == "x":
+                a = ch[1]
+                raws[ch] = xin.tile([P, PACK, T], F32, name="x_raw")
+                nc.sync.dma_start(raws[ch][:], xT[a * K_PASS : (a + 1) * K_PASS, :].rearrange("(p t) c -> p t c", t=PACK))
+            elif ch[0] == "w":
+                e, a, lo, hi = ch[1:5]
+                raws[ch] = w_in.tile([P, PACK, hi - lo], F32, name="w_raw")
+                nc.sync.dma_start(
+                    raws[ch][:], w[e, a * K_PASS : (a + 1) * K_PASS, lo:hi].rearrange("(p t) c -> p t c", t=PACK)
+                )
+            elif ch[0] == "offs":
+                nc.sync.dma_start(offsets[:], offs)
+            elif ch[0] == "bias":
+                nc.sync.dma_start(bias[:], b.rearrange("(c p) e -> p c e", p=P))
+            elif ch[0] == "gate":
+                nc.sync.dma_start(gates[:], gate[0:P, :])
+            elif ch[0] == "xr":
+                c = ch[1]
+                nc.sync.dma_start(residual[c][:], xr[c * P : (c + 1) * P, :])
+
+        def group(ch):
+            if ch[0] == "x":
+                g = xgrp.tile([P, PACK * T], BF16, name="x_grouped", align_bytes=64)
+                width, mid = T, 512
+            else:
+                width = ch[4] - ch[3]
+                mid = ch[5]
+                g = wgrp.tile([P, PACK * width], BF16, name="w_grouped", align_bytes=64)
+            grps[ch] = g
+            if mid > 0:
+                interleave(scopy, g, raws[ch], 0, mid)
+            if mid < width:
+                interleave(vcopy, g, raws[ch], mid, width)
+
+        def quantize(ch):
+            g = grps[ch]
+            if ch[0] == "x":
+                a = ch[1]
+                for lo, hi in ((0, 512), (512, 768)):
+                    nc.vector.quantize_mx(
+                        out=x_codes[a][:, lo:hi].bitcast(FP8X4), scales=x_scales[4 * a :, lo:hi], in_=g[:, PACK * lo : PACK * hi]
+                    )
+                return
+            e, a, base, end = ch[1:5]
+            if (e, a) not in w_codes:
+                w_codes[e, a] = wq.tile([P, N], U32, name="w_codes", align_bytes=64)
+                w_scales[e, a] = wq.tile([P, N], U8, name="w_scales", align_bytes=64)
+            cuts = ((0, 256), (256, 384)) if end - base == 384 else ((0, end - base),)
+            for lo, hi in cuts:
+                cols = slice(base + lo, base + hi)
+                nc.vector.quantize_mx(
+                    out=w_codes[e, a][:, cols].bitcast(FP8X4), scales=w_scales[e, a][:, cols], in_=g[:, PACK * lo : PACK * hi]
+                )
+
+        def finish(ch):
+            if ch[0] == "x":
+                a = ch[1]
+                nc.vector.tensor_copy(slot_codes[a][:], x_codes[a][:].indirect(offsets[:]))
+                if a == PASSES - 1:
+                    nc.vector.tensor_copy(slot_scales[:], x_scales[:].indirect(offsets[:]))
+                return
+            e, a, base, end = ch[1:5]
+            slots = slice(e * C, (e + 1) * C)
+            for c in range(base // P, end // P):
+                if a == 0:
+                    acc[e, c] = psum.tile([P, C], F32, name=f"acc{c}")
+                cols = slice(c * P, (c + 1) * P)
+                nc.tensor.matmul_mx(
+                    out=acc[e, c][:],
+                    lhsT=w_codes[e, a][:, cols].bitcast(FP8X4),
+                    lhsT_scale=w_scales[e, a][:, cols],
+                    rhs=slot_codes[a][:, slots].bitcast(FP8X4),
+                    rhs_scale=slot_scales[4 * a :, slots],
+                    start=(a == 0),
+                    stop=(a == PASSES - 1),
+                )
+                if a == PASSES - 1:
+                    y = ypool.tile([P, C], F32, name="y")
+                    nc.scalar.activation(y[:], acc[e, c][:], IDENTITY, bias=bias[:, c, e : e + 1])
+                    nc.vector.tensor_tensor(
+                        window[c][:].indirect(offsets[:, e * 8 : (e + 1) * 8]), y[:], gates[:, slots], MULT
+                    )
+                    if e == E - 1:
+                        nc.vector.tensor_add(result[c][:], residual[c][:], window[c][:])
+                        nc.sync.dma_start(out[c * P : (c + 1) * P, :], result[c][:])
+
+        chunks = [("x", 0), ("offs",), ("x", 1), ("x", 2), ("x", 3), ("bias",), ("gate",)]
+        for e in range(E):
+            for a in range(PASSES):
+                if (e, a) == (E - 1, PASSES - 1):
+                    chunks += [("w", e, a, 0, 256, 128), ("xr", 0), ("xr", 1), ("w", e, a, 256, 384, 128), ("xr", 2)]
+                else:
+                    chunks.append(("w", e, a, 0, N, 256))
+        ahead = 8
+        work = [ch for ch in chunks if ch[0] in "xw"]
+        loaded = 0
+        for i in range(len(work) + 2):
+            target = chunks.index(work[min(i + ahead, len(work) - 1)]) + 1
+            if i + ahead >= len(work):
+                target = len(chunks)
+            while loaded < target:
+                load(chunks[loaded])
+                loaded += 1
+            if i < len(work):
+                group(work[i])
+            if 1 <= i <= len(work):
+                quantize(work[i - 1])
+            if i >= 2:
+                finish(work[i - 2])

@@ -12,6 +12,7 @@ FP8X4 = mybir.dt.float8_e4m3fn_x4
 COPY = mybir.ActivationFunctionType.Copy
 IDENTITY = mybir.ActivationFunctionType.Identity
 MULT = mybir.AluOpType.mult
+ADD = mybir.AluOpType.add
 
 P = 128
 PACK = 4
@@ -35,9 +36,9 @@ def tile_moe_res_lin_bias_kernel(tc, xT, xr, w, b, gate, offs, out):
     with (
         tc.tile_pool(name="held", bufs=1) as held,
         tc.tile_pool(name="xin", bufs=4) as xin,
-        tc.tile_pool(name="win", bufs=12) as w_in,
+        tc.tile_pool(name="win", bufs=1) as w_in,
         tc.tile_pool(name="xgrp", bufs=2) as xgrp,
-        tc.tile_pool(name="wgrp", bufs=4) as wgrp,
+        tc.tile_pool(name="wgrp", bufs=3) as wgrp,
         tc.tile_pool(name="wq", bufs=8) as wq,
         tc.tile_pool(name="ypool", bufs=4) as ypool,
         tc.psum_pool(name="acc", bufs=2) as psum,
@@ -47,7 +48,6 @@ def tile_moe_res_lin_bias_kernel(tc, xT, xr, w, b, gate, offs, out):
         gates = held.tile([P, S], F32, name="gates")
         residual = [held.tile([P, T], F32, name=f"residual{c}") for c in range(BLOCKS)]
         window = [held.tile([P, T], F32, name=f"window{c}") for c in range(BLOCKS)]
-        result = [held.tile([P, T], F32, name=f"result{c}") for c in range(BLOCKS)]
         x_codes = [held.tile([P, T], U32, name=f"x_codes{a}", align_bytes=64) for a in range(PASSES)]
         x_scales = held.tile([P, T], U8, name="x_scales", align_bytes=64)
         slot_codes = [held.tile([P, S], U32, name=f"slot_codes{a}", align_bytes=64) for a in range(PASSES)]
@@ -61,19 +61,30 @@ def tile_moe_res_lin_bias_kernel(tc, xT, xr, w, b, gate, offs, out):
         scopy = lambda o, i: nc.scalar.activation(o, i, COPY)
 
         raws, grps = {}, {}
-        w_codes, w_scales, acc = {}, {}, {}
+        w_codes, w_scales, acc, ys = {}, {}, {}, {}
 
         def load(ch):
             if ch[0] == "x":
                 a = ch[1]
-                raws[ch] = xin.tile([P, PACK, T], F32, name="x_raw")
-                nc.sync.dma_start(raws[ch][:], xT[a * K_PASS : (a + 1) * K_PASS, :].rearrange("(p t) c -> p t c", t=PACK))
+                raw = xin.tile([P, PACK, T], F32, name="x_raw")
+                nc.sync.dma_start(raw[:], xT[a * K_PASS : (a + 1) * K_PASS, :].rearrange("(p t) c -> p t c", t=PACK))
+                raws[ch] = raw[:]
+            elif ch[0] == "pair":
+                e, a = ch[1:3]
+                raw = w_in.tile([P, 2, PACK, N], F32, name=f"w_raw{e}_{a}")
+                nc.sync.dma_start(
+                    raw[:].rearrange("p a t c -> p a (t c)"),
+                    w[e, a * K_PASS : (a + 2) * K_PASS, :].rearrange("(a p t) c -> p a (t c)", a=2, t=PACK),
+                )
+                raws[e, a, 0, N] = raw[:, 0, :, :]
+                raws[e, a + 1, 0, N] = raw[:, 1, :, :]
             elif ch[0] == "w":
                 e, a, lo, hi = ch[1:5]
-                raws[ch] = w_in.tile([P, PACK, hi - lo], F32, name="w_raw")
+                raw = w_in.tile([P, PACK, hi - lo], F32, name=f"w_raw{e}_{a}_{lo}")
                 nc.sync.dma_start(
-                    raws[ch][:], w[e, a * K_PASS : (a + 1) * K_PASS, lo:hi].rearrange("(p t) c -> p t c", t=PACK)
+                    raw[:], w[e, a * K_PASS : (a + 1) * K_PASS, lo:hi].rearrange("(p t) c -> p t c", t=PACK)
                 )
+                raws[e, a, lo, hi] = raw[:]
             elif ch[0] == "offs":
                 nc.sync.dma_start(offsets[:], offs)
             elif ch[0] == "bias":
@@ -87,16 +98,18 @@ def tile_moe_res_lin_bias_kernel(tc, xT, xr, w, b, gate, offs, out):
         def group(ch):
             if ch[0] == "x":
                 g = xgrp.tile([P, PACK * T], BF16, name="x_grouped", align_bytes=64)
-                width, mid = T, 512
+                width, mid = T, [512,512,512,512][ch[1]]
+                raw = raws[ch]
             else:
                 width = ch[4] - ch[3]
                 mid = ch[5]
                 g = wgrp.tile([P, PACK * width], BF16, name="w_grouped", align_bytes=64)
+                raw = raws[ch[1:5]]
             grps[ch] = g
             if mid > 0:
-                interleave(scopy, g, raws[ch], 0, mid)
+                interleave(scopy, g, raw, 0, mid)
             if mid < width:
-                interleave(vcopy, g, raws[ch], mid, width)
+                interleave(vcopy, g, raw, mid, width)
 
         def quantize(ch):
             g = grps[ch]
@@ -141,35 +154,50 @@ def tile_moe_res_lin_bias_kernel(tc, xT, xr, w, b, gate, offs, out):
                     stop=(a == PASSES - 1),
                 )
                 if a == PASSES - 1:
-                    y = ypool.tile([P, C], F32, name="y")
-                    nc.scalar.activation(y[:], acc[e, c][:], IDENTITY, bias=bias[:, c, e : e + 1])
-                    nc.vector.tensor_tensor(
-                        window[c][:].indirect(offsets[:, e * 8 : (e + 1) * 8]), y[:], gates[:, slots], MULT
-                    )
-                    if e == E - 1:
-                        nc.vector.tensor_add(result[c][:], residual[c][:], window[c][:])
-                        nc.sync.dma_start(out[c * P : (c + 1) * P, :], result[c][:])
+                    ys[e, c] = ypool.tile([P, C], F32, name="y")
+                    nc.vector.scalar_tensor_tensor(ys[e, c][:], acc[e, c][:], bias[:, c, e : e + 1], gates[:, slots], ADD, MULT)
 
-        chunks = [("x", 0), ("offs",), ("x", 1), ("x", 2), ("x", 3), ("bias",), ("gate",)]
+        def scatter(ch):
+            if ch[0] == "x" or ch[2] < PASSES - 1:
+                return
+            e, a, base, end = ch[1:5]
+            slots = slice(e * C, (e + 1) * C)
+            for c in range(base // P, end // P):
+                target = window[c][:].indirect(offsets[:, e * 8 : (e + 1) * 8])
+                nc.vector.tensor_copy(target, ys[e, c][:])
+
+        def add_and_store(c, parts):
+            for h in range(parts):
+                cs = slice(h * T // parts, (h + 1) * T // parts)
+                engine = nc.gpsimd if c in [] else nc.vector
+                engine.tensor_tensor(residual[c][:, cs], residual[c][:, cs], window[c][:, cs], ADD)
+                nc.sync.dma_start(out[c * P : (c + 1) * P, cs], residual[c][:, cs])
+
+        mids = [256,384,256,256]
+        loads = [("x", 0), ("offs",), ("x", 1), ("x", 2), ("x", 3), ("bias",), ("gate",)]
+        work = [("x", a) for a in range(PASSES)]
+        last = E - 1
         for e in range(E):
             for a in range(PASSES):
-                if (e, a) == (E - 1, PASSES - 1):
-                    chunks += [("w", e, a, 0, 256, 128), ("xr", 0), ("xr", 1), ("w", e, a, 256, 384, 128), ("xr", 2)]
-                else:
-                    chunks.append(("w", e, a, 0, N, 256))
-        ahead = 8
-        work = [ch for ch in chunks if ch[0] in "xw"]
-        loaded = 0
-        for i in range(len(work) + 2):
-            target = chunks.index(work[min(i + ahead, len(work) - 1)]) + 1
-            if i + ahead >= len(work):
-                target = len(chunks)
-            while loaded < target:
-                load(chunks[loaded])
-                loaded += 1
+                if e < last or a < 2:
+                    work.append(("w", e, a, 0, N, mids[a]))
+                    if a % 2 == 0 and (e < last or a + 1 < 2):
+                        loads.append(("pair", e, a))
+                    elif a % 2 == 0:
+                        loads.append(("w", e, a, 0, N))
+        tail = [("w", 3, 2, 0, 256, 128), ("w", 3, 3, 0, 256, 128), ("w", 3, 2, 256, 384, 128), ("w", 3, 3, 256, 384, 128), ("xr", 0), ("xr", 1), ("xr", 2)]
+        loads += tail
+        work += [t for t in tail if t[0] == "w"]
+        for ch in loads:
+            load(ch)
+        for i in range(len(work) + 4):
             if i < len(work):
                 group(work[i])
             if 1 <= i <= len(work):
                 quantize(work[i - 1])
-            if i >= 2:
+            if 2 <= i <= len(work) + 1:
                 finish(work[i - 2])
+            if i >= 4:
+                scatter(work[i - 4])
+        for c in range(BLOCKS):
+            add_and_store(c, 2 if c == BLOCKS - 1 else 1)

@@ -98,7 +98,7 @@ def tile_moe_res_lin_bias_kernel(tc, xT, xr, w, b, gate, offs, out):
         def group(ch):
             if ch[0] == "x":
                 g = xgrp.tile([P, PACK * T], BF16, name="x_grouped", align_bytes=64)
-                width, mid = T, [512,512,512,512][ch[1]]
+                width, mid = T, [512,640,640,640][ch[1]]
                 raw = raws[ch]
             else:
                 width = ch[4] - ch[3]
@@ -173,19 +173,19 @@ def tile_moe_res_lin_bias_kernel(tc, xT, xr, w, b, gate, offs, out):
                 engine.tensor_tensor(residual[c][:, cs], residual[c][:, cs], window[c][:, cs], ADD)
                 nc.sync.dma_start(out[c * P : (c + 1) * P, cs], residual[c][:, cs])
 
-        mids = [256,384,256,256]
+        mids = [256,384,384,384]
         loads = [("x", 0), ("offs",), ("x", 1), ("x", 2), ("x", 3), ("bias",), ("gate",)]
         work = [("x", a) for a in range(PASSES)]
         last = E - 1
         for e in range(E):
             for a in range(PASSES):
-                if e < last or a < 2:
+                if e < last or a < 3:
                     work.append(("w", e, a, 0, N, mids[a]))
-                    if a % 2 == 0 and (e < last or a + 1 < 2):
+                    if a % 2 == 0 and (e < last or a + 1 < 3):
                         loads.append(("pair", e, a))
                     elif a % 2 == 0:
                         loads.append(("w", e, a, 0, N))
-        tail = [("w", 3, 2, 0, 256, 128), ("w", 3, 3, 0, 256, 128), ("w", 3, 2, 256, 384, 128), ("w", 3, 3, 256, 384, 128), ("xr", 0), ("xr", 1), ("xr", 2)]
+        tail = [("w", 3, 3, 0, 256, 128), ("w", 3, 3, 256, 384, 128), ("xr", 0), ("xr", 1), ("xr", 2)]
         loads += tail
         work += [t for t in tail if t[0] == "w"]
         for ch in loads:

import concourse.mybir as mybir

K, T, E, C, N = 2048, 768, 4, 128, 384
S = E * C

F32 = mybir.dt.float32
BF16 = mybir.dt.bfloat16
U32 = mybir.dt.uint32
U16 = mybir.dt.uint16
U8 = mybir.dt.uint8
FP8X4 = mybir.dt.float8_e4m3fn_x4
COPY = mybir.ActivationFunctionType.Copy
IDENTITY = mybir.ActivationFunctionType.Identity
MULT = mybir.AluOpType.mult
ADD = mybir.AluOpType.add

P = 128
PACK = 4
K_PASS = P * PACK
PASSES = K // K_PASS
BLOCKS = N // P

FLOPS = 2 * S * K * N
BYTES = 4 * (K * T + 2 * N * T + E * K * N + N * E + S) + 2 * S


def interleave(copy, grouped, raw, lo, hi):
    copy(
        grouped[:, PACK * lo : PACK * hi].rearrange("p (c i t) -> p c t i", i=4, t=PACK),
        raw[:, :, lo:hi].rearrange("p t (c i) -> p c t i", i=4),
    )


def tile_moe_res_lin_bias_kernel(tc, xT, xr, w, b, gate, offs, out):
    nc = tc.nc
    with (
        tc.tile_pool(name="held", bufs=1) as held,
        tc.tile_pool(name="xin", bufs=4) as xin,
        tc.tile_pool(name="win", bufs=1) as w_in,
        tc.tile_pool(name="xgrp", bufs=2) as xgrp,
        tc.tile_pool(name="wgrp", bufs=3) as wgrp,
        tc.tile_pool(name="wq", bufs=8) as wq,
        tc.tile_pool(name="ypool", bufs=4) as ypool,
        tc.psum_pool(name="acc", bufs=2) as psum,
    ):
        offsets = held.tile([P, S // 16], U16, name="offsets")
        bias = held.tile([P, BLOCKS, E], F32, name="bias")
        gates = held.tile([P, S], F32, name="gates")
        residual = [held.tile([P, T], F32, name=f"residual{c}") for c in range(BLOCKS)]
        window = [held.tile([P, T], F32, name=f"window{c}") for c in range(BLOCKS)]
        x_codes = [held.tile([P, T], U32, name=f"x_codes{a}", align_bytes=64) for a in range(PASSES)]
        x_scales = held.tile([P, T], U8, name="x_scales", align_bytes=64)
        slot_codes = [held.tile([P, S], U32, name=f"slot_codes{a}", align_bytes=64) for a in range(PASSES)]
        slot_scales = held.tile([P, S], U8, name="slot_scales", align_bytes=64)

        nc.gpsimd.memset(x_scales[:], 0)
        for c in range(BLOCKS):
            nc.gpsimd.memset(window[c][:], 0.0)

        vcopy = lambda o, i: nc.vector.tensor_copy(o, i)
        scopy = lambda o, i: nc.scalar.activation(o, i, COPY)

        raws, grps = {}, {}
        w_codes, w_scales, acc, ys = {}, {}, {}, {}

        def load(ch):
            if ch[0] == "x":
                a = ch[1]
                raw = xin.tile([P, PACK, T], F32, name="x_raw")
                nc.sync.dma_start(raw[:], xT[a * K_PASS : (a + 1) * K_PASS, :].rearrange("(p t) c -> p t c", t=PACK))
                raws[ch] = raw[:]
            elif ch[0] == "pair":
                e, a = ch[1:3]
                raw = w_in.tile([P, 2, PACK, N], F32, name=f"w_raw{e}_{a}")
                nc.sync.dma_start(
                    raw[:].rearrange("p a t c -> p a (t c)"),
                    w[e, a * K_PASS : (a + 2) * K_PASS, :].rearrange("(a p t) c -> p a (t c)", a=2, t=PACK),
                )
                raws[e, a, 0, N] = raw[:, 0, :, :]
                raws[e, a + 1, 0, N] = raw[:, 1, :, :]
            elif ch[0] == "w":
                e, a, lo, hi = ch[1:5]
                raw = w_in.tile([P, PACK, hi - lo], F32, name=f"w_raw{e}_{a}_{lo}")
                nc.sync.dma_start(
                    raw[:], w[e, a * K_PASS : (a + 1) * K_PASS, lo:hi].rearrange("(p t) c -> p t c", t=PACK)
                )
                raws[e, a, lo, hi] = raw[:]
            elif ch[0] == "offs":
                nc.sync.dma_start(offsets[:], offs)
            elif ch[0] == "bias":
                nc.sync.dma_start(bias[:], b.rearrange("(c p) e -> p c e", p=P))
            elif ch[0] == "gate":
                nc.sync.dma_start(gates[:], gate[0:P, :])
            elif ch[0] == "xr":
                c = ch[1]
                nc.sync.dma_start(residual[c][:], xr[c * P : (c + 1) * P, :])

        def group(ch):
            if ch[0] == "x":
                g = xgrp.tile([P, PACK * T], BF16, name="x_grouped", align_bytes=64)
                width, mid = T, [512,640,640,640][ch[1]]
                raw = raws[ch]
            else:
                width = ch[4] - ch[3]
                mid = ch[5]
                g = wgrp.tile([P, PACK * width], BF16, name="w_grouped", align_bytes=64)
                raw = raws[ch[1:5]]
            grps[ch] = g
            if mid > 0:
                interleave(scopy, g, raw, 0, mid)
            if mid < width:
                interleave(vcopy, g, raw, mid, width)

        def quantize(ch):
            g = grps[ch]
            if ch[0] == "x":
                a = ch[1]
                for lo, hi in ((0, 512), (512, 768)):
                    nc.vector.quantize_mx(
                        out=x_codes[a][:, lo:hi].bitcast(FP8X4), scales=x_scales[4 * a :, lo:hi], in_=g[:, PACK * lo : PACK * hi]
                    )
                return
            e, a, base, end = ch[1:5]
            if (e, a) not in w_codes:
                w_codes[e, a] = wq.tile([P, N], U32, name="w_codes", align_bytes=64)
                w_scales[e, a] = wq.tile([P, N], U8, name="w_scales", align_bytes=64)
            cuts = ((0, 256), (256, 384)) if end - base == 384 else ((0, end - base),)
            for lo, hi in cuts:
                cols = slice(base + lo, base + hi)
                nc.vector.quantize_mx(
                    out=w_codes[e, a][:, cols].bitcast(FP8X4), scales=w_scales[e, a][:, cols], in_=g[:, PACK * lo : PACK * hi]
                )

        def finish(ch):
            if ch[0] == "x":
                a = ch[1]
                nc.vector.tensor_copy(slot_codes[a][:], x_codes[a][:].indirect(offsets[:]))
                if a == PASSES - 1:
                    nc.vector.tensor_copy(slot_scales[:], x_scales[:].indirect(offsets[:]))
                return
            e, a, base, end = ch[1:5]
            slots = slice(e * C, (e + 1) * C)
            for c in range(base // P, end // P):
                if a == 0:
                    acc[e, c] = psum.tile([P, C], F32, name=f"acc{c}")
                cols = slice(c * P, (c + 1) * P)
                nc.tensor.matmul_mx(
                    out=acc[e, c][:],
                    lhsT=w_codes[e, a][:, cols].bitcast(FP8X4),
                    lhsT_scale=w_scales[e, a][:, cols],
                    rhs=slot_codes[a][:, slots].bitcast(FP8X4),
                    rhs_scale=slot_scales[4 * a :, slots],
                    start=(a == 0),
                    stop=(a == PASSES - 1),
                )
                if a == PASSES - 1:
                    ys[e, c] = ypool.tile([P, C], F32, name="y")
                    nc.vector.scalar_tensor_tensor(ys[e, c][:], acc[e, c][:], bias[:, c, e : e + 1], gates[:, slots], ADD, MULT)

        def scatter(ch):
            if ch[0] == "x" or ch[2] < PASSES - 1:
                return
            e, a, base, end = ch[1:5]
            slots = slice(e * C, (e + 1) * C)
            for c in range(base // P, end // P):
                target = window[c][:].indirect(offsets[:, e * 8 : (e + 1) * 8])
                nc.vector.tensor_copy(target, ys[e, c][:])

        def add_and_store(c, parts):
            for h in range(parts):
                cs = slice(h * T // parts, (h + 1) * T // parts)
                engine = nc.gpsimd if c in [] else nc.vector
                engine.tensor_tensor(residual[c][:, cs], residual[c][:, cs], window[c][:, cs], ADD)
                nc.sync.dma_start(out[c * P : (c + 1) * P, cs], residual[c][:, cs])

        mids = [256,384,384,384]
        loads = [("x", 0), ("offs",), ("x", 1), ("x", 2), ("x", 3), ("bias",), ("gate",)]
        work = [("x", a) for a in range(PASSES)]
        last = E - 1
        for e in range(E):
            for a in range(PASSES):
                if e < last or a < 3:
                    work.append(("w", e, a, 0, N, mids[a]))
                    if a % 2 == 0 and (e < last or a + 1 < 3):
                        loads.append(("pair", e, a))
                    elif a % 2 == 0:
                        loads.append(("w", e, a, 0, N))
        tail = [("w", 3, 3, 0, 256, 128), ("w", 3, 3, 256, 384, 128), ("xr", 0), ("xr", 1), ("xr", 2)]
        loads += tail
        work += [t for t in tail if t[0] == "w"]
        for ch in loads:
            load(ch)
        for i in range(len(work) + 4):
            if i < len(work):
                group(work[i])
            if 1 <= i <= len(work):
                quantize(work[i - 1])
            if 2 <= i <= len(work) + 1:
                finish(work[i - 2])
            if i >= 4:
                scatter(work[i - 4])
        for c in range(BLOCKS):
            add_and_store(c, 2 if c == BLOCKS - 1 else 1)
